import numpy as np
import ml_dtypes


def mxq(x, axis, fmt="e4m3"):
    dtype, down = {"e4m3": (ml_dtypes.float8_e4m3fn, 7), "e5m2": (ml_dtypes.float8_e5m2, 14)}[fmt]
    v = np.moveaxis(np.asarray(x, np.float32).astype(ml_dtypes.bfloat16).astype(np.float64), axis, -1)
    blocks = v.reshape(v.shape[:-1] + (-1, 32))
    amax = np.abs(blocks).max(-1, keepdims=True)
    byte = np.maximum(np.where(amax > 0, np.frexp(amax)[1] - 1 + 127, 0) - down, 1)
    scale = np.exp2(byte - 127.0)
    codes = (blocks / scale).astype(np.float32).astype(dtype).astype(np.float64)
    return np.moveaxis((codes * scale).reshape(v.shape), -1, axis)


WIDE = False


def mx_kscale(k):
    if not WIDE:
        return np.ones(k)
    levels = np.array([10, -10, 5, -5, 0])
    if k % 512:
        return np.exp2(np.random.permutation(np.resize(levels, k // 32))).repeat(32)
    a = np.empty((k // 512, 16))
    for p in range(k // 512):
        a[p, :8] = np.random.permutation(np.resize(levels, 8))
        for g in range(8):
            far = levels[np.abs(levels - a[p, g]) >= 10]
            a[p, g + 8] = far[np.random.randint(len(far))]
    return np.exp2(a.ravel()).repeat(32)


def f64(x):
    return np.asarray(x).astype(np.float64)


def striped(idx):
    return np.tile(np.asarray(idx).reshape(-1, 16).T, (8, 1)).astype(np.uint16)


def unstriped(offs):
    return offs[:16].T.reshape(-1).astype(np.int64)


E2M1 = np.array([0.0, 0.5, 1.0, 1.5, 2.0, 3.0, 4.0, 6.0, -0.0, -0.5, -1.0, -1.5, -2.0, -3.0, -4.0, -6.0])


def pack_weight(w, fmt):
    k, n = w.shape
    w = f64(np.asarray(w, np.float32).astype(ml_dtypes.bfloat16)).reshape(k // 32, 32, n)
    amax = np.abs(w).max(1)
    if fmt == "e4m3":
        byte = np.frexp(amax)[1] - 1 + 127 - 7
    else:
        mant, ex = np.frexp(amax / 6.0)
        byte = np.where(mant > 0.5, ex, ex - 1) + 127
    byte = np.clip(np.where(amax > 0, byte, 1), 1, 254)
    scaled = (w * np.exp2(127.0 - byte)[:, None, :]).reshape(k, n).astype(np.float32)
    by_word = np.ascontiguousarray(scaled.reshape(k // 512, 128, 4, n).transpose(0, 1, 3, 2))
    if fmt == "e4m3":
        words = by_word.astype(ml_dtypes.float8_e4m3fn).view(np.uint8)
    else:
        c = by_word.astype(ml_dtypes.float4_e2m1fn).view(np.uint8) & 0xF
        words = (c[..., 0::2] | (c[..., 1::2] << 4)).reshape(k // 512, 128, 2 * n)
    return np.ascontiguousarray(words), np.ascontiguousarray(byte.astype(np.uint8).reshape(k // 512, 16, n))


def unpack_weight(words, scales, fmt):
    g, _, n = scales.shape
    words = np.ascontiguousarray(words).reshape(g, 128, n, -1)
    if fmt == "e4m3":
        vals = words.view(ml_dtypes.float8_e4m3fn).astype(np.float64)
    else:
        nib = np.empty((g, 128, n, 4), np.uint8)
        nib[..., 0::2] = words & 0xF
        nib[..., 1::2] = words >> 4
        vals = E2M1[nib]
    vals = vals * np.repeat(np.exp2(scales.astype(np.float64) - 127.0), 8, axis=1)[..., None]
    return vals.transpose(0, 1, 3, 2).reshape(g * 512, n)


def bf(x):
    return np.asarray(x, np.float32).astype(ml_dtypes.bfloat16)


def planes(Y):
    r, m = Y.shape
    b = f64(bf(Y)).reshape(r // 32, 32, m)
    amax = np.abs(b).max(1)
    byte = np.clip(np.where(amax > 0, np.frexp(amax)[1] - 1 + 127 - 7, 1), 1, 254)
    codes = (b * np.exp2(127.0 - byte)[:, None, :]).reshape(r, m).astype(np.float32).astype(ml_dtypes.float8_e4m3fn).view(np.uint8)
    words = codes.reshape(r // 512, 128, 4, m).transpose(0, 1, 3, 2)
    return np.ascontiguousarray(words), np.ascontiguousarray(byte.astype(np.uint8).reshape(r // 512, 16, m))


D, T, I, Q, E, N, H = 512, 2048, 512, 256, 512, 32, 32


def setup_inputs():
    n = np.random.standard_normal
    idx = np.random.permutation(T)[:I]
    fd = mx_kscale(D)
    fi = mx_kscale(I)
    keysp = pack_weight(n((D, T)) / fd[:, None], "e2m1")
    return {
        "query": (n((D, Q)) * 0.7 / np.sqrt(D) * fd[:, None]).astype(np.float32),
        "query2": (n((D, Q)) * 0.9 / np.sqrt(D) * fd[:, None]).astype(np.float32),
        "keys_words": keysp[0],
        "keys_scales": keysp[1],
        "lam": (np.random.uniform(0.3, 0.9, (Q, 1))).astype(np.float32),
        "reserve": (np.random.uniform(0.5, 2.0, (Q, 1))).astype(np.float32),
        "os": (np.random.uniform(4.0, 16.0, (1, I)) * fi).astype(np.float32),
        "vals": (n((E, T))).astype(np.float32),
        "vsc": (np.random.uniform(0.5, 2.0, (1, I)) / fi).astype(np.float32),
        "offs": striped(idx),
    }


def reference(query, query2, keys_words, keys_scales, lam, reserve, os, vals, vsc, offs):
    idx = unstriped(offs)
    keysu = unpack_weight(keys_words, keys_scales, "e2m1")
    queryq = mxq(f64(query), 0, "e4m3")
    keysidxg = keysu[:, idx]
    a = queryq.T @ keysidxg
    query2q = mxq(f64(query2), 0, "e4m3")
    b = query2q.T @ keysidxg
    mb = b.reshape(Q, N, I // N).max(axis=2)
    mr = np.repeat(mb, I // N, axis=1)
    s = a + mr * f64(lam)
    p = np.exp(s - np.max(s, axis=1, keepdims=True))
    r = p / np.sum(p, axis=1, keepdims=True)
    u0 = r * np.log(r) * (-1.0)
    w = u0 / (np.sum(u0, axis=1, keepdims=True) + f64(reserve))
    wo1 = w * f64(os)
    wt1 = wo1.T
    vg = f64(vals)[:, idx].reshape(E, H, I // H).mean(axis=2)
    vgr = np.repeat(vg, I // H, axis=1)
    vd = (f64(vals)[:, idx] - vgr) * f64(vsc)
    vt1 = vd.T
    vt1q = mxq(vt1, 0, "e4m3")
    wt1q = mxq(wt1, 0, "e4m3")
    o = vt1q.T @ wt1q
    words, scales = planes(o)
    return o, words, scales

@@ -1,0 +1,304 @@
+from contextlib import ExitStack
+
+import concourse.mybir as mybir
+from concourse.masks import make_identity
+
+D, T, I, Q, E = 512, 2048, 512, 256, 512
+P = 128
+PACK = 4
+PAGE = 16
+PAGES = I // PAGE
+QT = Q // P
+
+F32 = mybir.dt.float32
+BF16 = mybir.dt.bfloat16
+I32 = mybir.dt.int32
+U32 = mybir.dt.uint32
+U16 = mybir.dt.uint16
+U8 = mybir.dt.uint8
+FP8X4 = mybir.dt.float8_e4m3fn_x4
+FP4X4 = mybir.dt.float4_e2m1fn_x4
+ALU = mybir.AluOpType
+ACT = mybir.ActivationFunctionType
+AX = mybir.AxisListType
+
+FLOPS = 2 * 2 * D * Q * I + 2 * I * E * Q
+
+
+def tile_attend_pagelift_lacking_centredvalues_pl_kernel(
+    tc, query, query2, keys_words, keys_scales, lam, reserve, os_row, vals, vsc, offs, out_0, out_1, out_2
+):
+    nc = tc.nc
+    with ExitStack() as ctx:
+        sb = ctx.enter_context(tc.tile_pool(name="sb", bufs=1))
+        ps = ctx.enter_context(tc.psum_pool(name="ps", bufs=1))
+
+        offsets = sb.tile([P, I // 16], U16, name="offsets")
+        nc.sync.dma_start(offsets[:], offs)
+
+        key_words = sb.tile([P, T], U16, name="key_words", align_bytes=64)
+        nc.sync.dma_start(out=key_words[:].bitcast(I32), in_=keys_words[0].bitcast(I32))
+
+        key_scales = sb.tile([P, T], U8, name="key_scales", align_bytes=64)
+        nc.vector.memset(key_scales[:].bitcast(I32), 0)
+        for quad in range(4):
+            nc.sync.dma_start(
+                out=key_scales[32 * quad : 32 * quad + 4, :].bitcast(I32),
+                in_=keys_scales[0, 4 * quad : 4 * quad + 4, :].bitcast(I32),
+            )
+
+        q_raw = []
+        for n, src in enumerate((query2, query)):
+            raw = sb.tile([P, PACK, Q], F32, name="q_raw%d" % n, align_bytes=64)
+            nc.sync.dma_start(out=raw[:], in_=src.rearrange("(p t) q -> p t q", t=PACK))
+            q_raw.append(raw)
+
+        val_pool = []
+        for j in range(PACK):
+            pool_j = sb.tile([P, T], F32, name="val_pool%d" % j, align_bytes=64)
+            nc.sync.dma_start(out=pool_j[:], in_=vals.rearrange("(p j) t -> j p t", j=PACK)[j])
+            val_pool.append(pool_j)
+
+        ident = sb.tile([P, P], F32, name="ident", align_bytes=64)
+        make_identity(nc, ident[:])
+
+        lam_col = sb.tile([P, QT], F32, name="lam_col")
+        res_col = sb.tile([P, QT], F32, name="res_col")
+        os_col = sb.tile([P, PACK], F32, name="os_col")
+        vsc_col = sb.tile([P, PACK], F32, name="vsc_col")
+        with nc.allow_non_contiguous_dma(reason="one value a partition"):
+            nc.gpsimd.dma_start(out=lam_col[:], in_=lam.rearrange("(h p) o -> p (h o)", p=P))
+            nc.gpsimd.dma_start(out=vsc_col[:], in_=vsc.rearrange("o (p t) -> p (o t)", t=PACK))
+            nc.gpsimd.dma_start(out=res_col[:], in_=reserve.rearrange("(h p) o -> p (h o)", p=P))
+            nc.gpsimd.dma_start(out=os_col[:], in_=os_row.rearrange("o (p t) -> p (o t)", t=PACK))
+
+        kg_words = sb.tile([P, I], U16, name="kg_words", align_bytes=64)
+        kg_scales = sb.tile([P, I], U8, name="kg_scales", align_bytes=64)
+        nc.vector.tensor_copy(kg_words[:], key_words[:].indirect(offsets[:]))
+        nc.vector.tensor_copy(kg_scales[:], key_scales[:].indirect(offsets[:]))
+
+        q_codes, q_scales = [], []
+        for n in range(2):
+            grouped = sb.tile([P, Q, PACK], BF16, name="q_grouped%d" % n, align_bytes=64)
+            nc.scalar.activation(
+                out=grouped[:].rearrange("p (c i) t -> p c t i", i=4),
+                in_=q_raw[n][:].rearrange("p t (c i) -> p c t i", i=4),
+                func=ACT.Copy,
+            )
+            codes = sb.tile([P, Q], U32, name="q_codes%d" % n, align_bytes=64)
+            scales = sb.tile([P, Q], U8, name="q_scales%d" % n, align_bytes=64)
+            nc.vector.quantize_mx(
+                out=codes[:].bitcast(FP8X4), scales=scales[:], in_=grouped[:].rearrange("p q t -> p (q t)")
+            )
+            q_codes.append(codes)
+            q_scales.append(scales)
+
+        def score(n, h, tag):
+            bank = ps.tile([P, I], F32, name="score", tag=tag)
+            cols = slice(h * P, (h + 1) * P)
+            nc.tensor.matmul_mx(
+                out=bank[:],
+                lhsT=q_codes[n][:, cols].bitcast(FP8X4),
+                lhsT_scale=q_scales[n][:, cols],
+                rhs=kg_words[:].bitcast(FP4X4),
+                rhs_scale=kg_scales[:],
+                start=True,
+                stop=True,
+            )
+            return bank
+
+        b_ps = [score(0, h, "b%d" % h) for h in range(QT)]
+        a_ps = [score(1, h, "a%d" % h) for h in range(QT)]
+
+        os_ps = ps.tile([P, PACK, P], F32, name="os_ps")
+        for t in range(PACK):
+            nc.tensor.transpose(os_ps[:, t, :], os_col[:, t : t + 1].to_broadcast([P, P]), ident[:])
+
+        page_max, s_sb, p_sb, neg_max = [], [], [], []
+        z_sum = sb.tile([P, QT], F32, name="z_sum")
+        for h in range(QT):
+            mb = sb.tile([P, PAGES], F32, name="page_max%d" % h)
+            nc.vector.tensor_reduce(
+                out=mb[:], in_=b_ps[h][:].rearrange("p (n k) -> p n k", k=PAGE), axis=AX.X, op=ALU.max
+            )
+            page_max.append(mb)
+        for h in range(QT):
+            s = sb.tile([P, I], F32, name="s%d" % h, align_bytes=64)
+            nc.vector.scalar_tensor_tensor(
+                out=s[:].rearrange("p (n k) -> p n k", k=PAGE),
+                in0=page_max[h][:].unsqueeze(2).to_broadcast([P, PAGES, PAGE]),
+                scalar=lam_col[:, h : h + 1],
+                in1=a_ps[h][:].rearrange("p (n k) -> p n k", k=PAGE),
+                op0=ALU.mult,
+                op1=ALU.add,
+            )
+            s_sb.append(s)
+        neg_max = sb.tile([P, QT], F32, name="neg_max")
+        for h in range(QT):
+            nc.vector.tensor_reduce(out=neg_max[:, h : h + 1], in_=s_sb[h][:], axis=AX.X, op=ALU.max, negate=True)
+
+        v_codes = sb.tile([P, PACK, P], U32, name="v_codes", align_bytes=64)
+        v_scales = sb.tile([P, PACK, P], U8, name="v_scales", align_bytes=64)
+
+        def gather_values(j):
+            g = sb.tile([P, I], F32, name="gathered%d" % j, align_bytes=64)
+            nc.scalar.activation(out=g[:], in_=val_pool[j][:].indirect(offsets[:]), func=ACT.Copy)
+            return g
+
+        def centre_values(j, g):
+            sums = sb.tile([P, PAGES], F32, name="sums%d" % j)
+            nc.vector.tensor_reduce(out=sums[:], in_=g[:].rearrange("p (n k) -> p n k", k=PAGE), axis=AX.X, op=ALU.add)
+            neg_mean = sb.tile([P, P], F32, name="neg_mean%d" % j, align_bytes=64)
+            nc.gpsimd.tensor_scalar(
+                out=neg_mean[:].rearrange("p (n r) -> p n r", r=PAGE // PACK),
+                in0=sums[:].unsqueeze(2).to_broadcast([P, PAGES, PAGE // PACK]),
+                scalar1=-1.0 / PAGE,
+                scalar2=0.0,
+                op0=ALU.mult,
+                op1=ALU.add,
+            )
+            turned = ps.tile([P, PACK, P], F32, name="turned", tag="turned", bufs=3)
+            for t in range(PACK):
+                nc.tensor.matmul(
+                    turned[:, t, :], lhsT=g[:, t:I:PACK], rhs=ident[:], is_transpose=True, start=(t == 0), stop=False
+                )
+            for t in range(PACK):
+                nc.tensor.matmul(
+                    turned[:, t, :],
+                    lhsT=neg_mean[:],
+                    rhs=ident[:],
+                    is_transpose=True,
+                    start=False,
+                    stop=(t == PACK - 1),
+                )
+            return turned
+
+        def scale_values(j, turned):
+            grouped = sb.tile([P, P, PACK], BF16, name="v_grouped%d" % j, align_bytes=64)
+            nc.vector.tensor_tensor(
+                out=grouped[:],
+                in0=turned[:].rearrange("p t e -> p e t"),
+                in1=vsc_col[:].unsqueeze(1).to_broadcast([P, P, PACK]),
+                op=ALU.mult,
+            )
+            return grouped
+
+        def quantise_values(j, grouped):
+            nc.vector.quantize_mx(
+                out=v_codes[:, j, :].bitcast(FP8X4),
+                scales=v_scales[:, j, :],
+                in_=grouped[:].rearrange("p e t -> p (e t)"),
+            )
+
+        g0 = gather_values(0)
+        for h in range(QT):
+            p = sb.tile([P, I], F32, name="p%d" % h, align_bytes=64)
+            nc.scalar.activation(
+                out=p[:], in_=s_sb[h][:], func=ACT.Exp, bias=neg_max[:, h : h + 1], accum_out=z_sum[:, h : h + 1]
+            )
+            p_sb.append(p)
+        g1 = gather_values(1)
+        t0 = centre_values(0, g0)
+        log_z = sb.tile([P, QT], F32, name="log_z")
+        nc.scalar.activation(out=log_z[:], in_=z_sum[:], func=ACT.Ln)
+        t1 = centre_values(1, g1)
+        z_res = sb.tile([P, QT], F32, name="z_res")
+        nc.vector.tensor_tensor(out=z_res[:], in0=z_sum[:], in1=res_col[:], op=ALU.mult)
+        vg0 = scale_values(0, t0)
+        shift = sb.tile([P, QT], F32, name="shift")
+        nc.vector.tensor_tensor(out=shift[:], in0=log_z[:], in1=neg_max[:], op=ALU.subtract)
+        quantise_values(0, vg0)
+        g2 = gather_values(2)
+        g3 = gather_values(3)
+
+        part_sum = sb.tile([P, QT], F32, name="part_sum")
+        parts = []
+        for h in range(QT):
+            part = sb.tile([P, I], F32, name="part%d" % h, align_bytes=64)
+            nc.vector.scalar_tensor_tensor(
+                out=part[:],
+                in0=s_sb[h][:],
+                scalar=shift[:, h : h + 1],
+                in1=p_sb[h][:],
+                op0=ALU.subtract,
+                op1=ALU.mult,
+                accum_out=part_sum[:, h : h + 1],
+            )
+            parts.append(part)
+        neg_den = sb.tile([P, QT], F32, name="neg_den")
+        nc.vector.tensor_tensor(out=neg_den[:], in0=part_sum[:], in1=z_res[:], op=ALU.subtract)
+        vg1 = scale_values(1, t1)
+        inv_den = sb.tile([P, QT], F32, name="inv_den")
+        nc.vector.reciprocal(out=inv_den[:], in_=neg_den[:])
+        quantise_values(1, vg1)
+        t2 = centre_values(2, g2)
+
+        w_codes = sb.tile([P, Q], U32, name="w_codes", align_bytes=64)
+        w_scales = sb.tile([P, Q], U8, name="w_scales", align_bytes=64)
+        w_grouped = []
+        for h in range(QT):
+            w = sb.tile([P, I], BF16, name="w%d" % h, align_bytes=64)
+            nc.vector.scalar_tensor_tensor(
+                out=w[:].rearrange("q (p t) -> q p t", t=PACK),
+                in0=parts[h][:].rearrange("q (p t) -> q p t", t=PACK),
+                scalar=inv_den[:, h : h + 1],
+                in1=os_ps[:].rearrange("q t p -> q p t"),
+                op0=ALU.mult,
+                op1=ALU.mult,
+            )
+            w_ps = ps.tile([P, 2, P], F32, name="w_ps", tag="a%d" % h)
+            words = w[:].bitcast(F32)
+            for u in range(2):
+                nc.tensor.transpose(w_ps[:, u, :], words[:, u : I // 2 : 2], ident[:])
+            grouped = sb.tile([P, P, PACK], BF16, name="w_grouped%d" % h, align_bytes=64)
+            nc.scalar.copy(out=grouped[:].bitcast(F32), in_=w_ps[:].rearrange("p u q -> p q u"))
+            w_grouped.append(grouped)
+        t3 = centre_values(3, g3)
+        vg2 = scale_values(2, t2)
+        for h in range(QT):
+            nc.vector.quantize_mx(
+                out=w_codes[:, h * P : (h + 1) * P].bitcast(FP8X4),
+                scales=w_scales[:, h * P : (h + 1) * P],
+                in_=w_grouped[h][:].rearrange("p q t -> p (q t)"),
+            )
+        quantise_values(2, vg2)
+        vg3 = scale_values(3, t3)
+        quantise_values(3, vg3)
+
+        y = sb.tile([P, PACK, Q], F32, name="y", align_bytes=64)
+        out_rows = out_0.rearrange("(p j) q -> p j q", j=PACK)
+        for half in range(2):
+            y_ps = ps.tile([P, 2, Q], F32, name="y_ps", tag="b%d" % half)
+            for r in range(2):
+                j = 2 * half + r
+                nc.tensor.matmul_mx(
+                    out=y_ps[:, r, :],
+                    lhsT=v_codes[:, j, :].bitcast(FP8X4),
+                    lhsT_scale=v_scales[:, j, :],
+                    rhs=w_codes[:].bitcast(FP8X4),
+                    rhs_scale=w_scales[:],
+                    start=True,
+                    stop=True,
+                )
+            nc.scalar.copy(out=y[:, 2 * half : 2 * half + 2, :], in_=y_ps[:])
+            nc.sync.dma_start(out=out_rows[:, 2 * half : 2 * half + 2, :], in_=y[:, 2 * half : 2 * half + 2, :])
+
+        y_grouped = sb.tile([P, Q, PACK], BF16, name="y_grouped", align_bytes=64)
+        nc.vector.tensor_copy(
+            out=y_grouped[:].rearrange("p (c i) j -> p c j i", i=4),
+            in_=y[:].rearrange("p j (c i) -> p c j i", i=4),
+        )
+        y_codes = sb.tile([P, Q], U32, name="y_codes", align_bytes=64)
+        y_scales = sb.tile([P, Q], U8, name="y_scales", align_bytes=64)
+        nc.vector.quantize_mx(
+            out=y_codes[:].bitcast(FP8X4), scales=y_scales[:], in_=y_grouped[:].rearrange("p q j -> p (q j)")
+        )
+        nc.sync.dma_start(
+            out=out_1[0].rearrange("p q r -> p (q r)").bitcast(I32), in_=y_codes[:].bitcast(I32)
+        )
+        for quad in range(4):
+            queue = nc.scalar if quad % 2 == 0 else nc.sync
+            queue.dma_start(
+                out=out_2[0, 4 * quad : 4 * quad + 4, :].bitcast(I32),
+                in_=y_scales[32 * quad : 32 * quad + 4, :].bitcast(I32),
+            )

@@ -40,7 +40,7 @@ def tile_attend_pagelift_lacking_centredvalues_pl_kernel(
         nc.sync.dma_start(out=key_words[:].bitcast(I32), in_=keys_words[0].bitcast(I32))
 
         key_scales = sb.tile([P, T], U8, name="key_scales", align_bytes=64)
-        nc.vector.memset(key_scales[:].bitcast(I32), 0)
+        nc.gpsimd.memset(key_scales[:].bitcast(I32), 0)
         for quad in range(4):
             nc.sync.dma_start(
                 out=key_scales[32 * quad : 32 * quad + 4, :].bitcast(I32),
@@ -49,28 +49,31 @@ def tile_attend_pagelift_lacking_centredvalues_pl_kernel(
 
         q_raw = []
         for n, src in enumerate((query2, query)):
-            raw = sb.tile([P, PACK, Q], F32, name="q_raw%d" % n, align_bytes=64)
+            raw = sb.tile([P, PACK, Q], F32, name="q_raw%d" % n, tag="q_raw%d" % n, align_bytes=64)
             nc.sync.dma_start(out=raw[:], in_=src.rearrange("(p t) q -> p t q", t=PACK))
             q_raw.append(raw)
-
-        val_pool = []
-        for j in range(PACK):
-            pool_j = sb.tile([P, T], F32, name="val_pool%d" % j, align_bytes=64)
-            nc.sync.dma_start(out=pool_j[:], in_=vals.rearrange("(p j) t -> j p t", j=PACK)[j])
-            val_pool.append(pool_j)
-
-        ident = sb.tile([P, P], F32, name="ident", align_bytes=64)
-        make_identity(nc, ident[:])
 
         lam_col = sb.tile([P, QT], F32, name="lam_col")
         res_col = sb.tile([P, QT], F32, name="res_col")
         os_col = sb.tile([P, PACK], F32, name="os_col")
         vsc_col = sb.tile([P, PACK], F32, name="vsc_col")
+
+        def load_values(j):
+            pool_j = sb.tile([P, T], F32, name="val_pool%d" % j, tag="val_pool%d" % j, align_bytes=64)
+            nc.sync.dma_start(out=pool_j[:], in_=vals.rearrange("(p j) t -> j p t", j=PACK)[j])
+            return pool_j
+
         with nc.allow_non_contiguous_dma(reason="one value a partition"):
-            nc.gpsimd.dma_start(out=lam_col[:], in_=lam.rearrange("(h p) o -> p (h o)", p=P))
-            nc.gpsimd.dma_start(out=vsc_col[:], in_=vsc.rearrange("o (p t) -> p (o t)", t=PACK))
-            nc.gpsimd.dma_start(out=res_col[:], in_=reserve.rearrange("(h p) o -> p (h o)", p=P))
-            nc.gpsimd.dma_start(out=os_col[:], in_=os_row.rearrange("o (p t) -> p (o t)", t=PACK))
+            nc.sync.dma_start(out=lam_col[:], in_=lam.rearrange("(h p) o -> p (h o)", p=P))
+        val_pool = [load_values(0)]
+        nc.sync.dma_start(out=vsc_col[:], in_=vsc.rearrange("o (p t) -> p (o t)", t=PACK))
+        nc.sync.dma_start(out=os_col[:], in_=os_row.rearrange("o (p t) -> p (o t)", t=PACK))
+        with nc.allow_non_contiguous_dma(reason="one value a partition"):
+            nc.sync.dma_start(out=res_col[:], in_=reserve.rearrange("(h p) o -> p (h o)", p=P))
+        val_pool.extend(load_values(j) for j in range(1, PACK))
+
+        ident = sb.tile([P, P], F32, name="ident", align_bytes=64)
+        make_identity(nc, ident[:])
 
         kg_words = sb.tile([P, I], U16, name="kg_words", align_bytes=64)
         kg_scales = sb.tile([P, I], U8, name="kg_scales", align_bytes=64)
@@ -79,17 +82,19 @@ def tile_attend_pagelift_lacking_centredvalues_pl_kernel(
 
         q_codes, q_scales = [], []
         for n in range(2):
-            grouped = sb.tile([P, Q, PACK], BF16, name="q_grouped%d" % n, align_bytes=64)
-            nc.scalar.activation(
-                out=grouped[:].rearrange("p (c i) t -> p c t i", i=4),
-                in_=q_raw[n][:].rearrange("p t (c i) -> p c t i", i=4),
-                func=ACT.Copy,
-            )
             codes = sb.tile([P, Q], U32, name="q_codes%d" % n, align_bytes=64)
             scales = sb.tile([P, Q], U8, name="q_scales%d" % n, align_bytes=64)
-            nc.vector.quantize_mx(
-                out=codes[:].bitcast(FP8X4), scales=scales[:], in_=grouped[:].rearrange("p q t -> p (q t)")
-            )
+            for h in range(QT):
+                cols = slice(h * P, (h + 1) * P)
+                grouped = sb.tile([P, P, PACK], BF16, name="q_grouped%d%d" % (n, h), align_bytes=64)
+                dst = grouped[:].rearrange("p (c i) t -> p c t i", i=4)
+                src = q_raw[n][:, :, cols].rearrange("p t (c i) -> p c t i", i=4)
+                nc.scalar.activation(out=dst, in_=src, func=ACT.Copy)
+                nc.vector.quantize_mx(
+                    out=codes[:, cols].bitcast(FP8X4),
+                    scales=scales[:, cols],
+                    in_=grouped[:].rearrange("p q t -> p (q t)"),
+                )
             q_codes.append(codes)
             q_scales.append(scales)
 
@@ -115,9 +120,9 @@ def tile_attend_pagelift_lacking_centredvalues_pl_kernel(
             nc.tensor.transpose(os_ps[:, t, :], os_col[:, t : t + 1].to_broadcast([P, P]), ident[:])
 
         page_max, s_sb, p_sb, neg_max = [], [], [], []
-        z_sum = sb.tile([P, QT], F32, name="z_sum")
+        z_sum = sb.tile([P, QT], F32, name="z_sum", tag="gathered2", align_bytes=64)
         for h in range(QT):
-            mb = sb.tile([P, PAGES], F32, name="page_max%d" % h)
+            mb = sb.tile([P, PAGES], F32, name="page_max%d" % h, tag="page_max%d" % h, align_bytes=64)
             nc.vector.tensor_reduce(
                 out=mb[:], in_=b_ps[h][:].rearrange("p (n k) -> p n k", k=PAGE), axis=AX.X, op=ALU.max
             )
@@ -133,34 +138,54 @@ def tile_attend_pagelift_lacking_centredvalues_pl_kernel(
                 op1=ALU.add,
             )
             s_sb.append(s)
-        neg_max = sb.tile([P, QT], F32, name="neg_max")
+        neg_max = sb.tile([P, QT], F32, name="neg_max", tag="gathered3", align_bytes=64)
         for h in range(QT):
             nc.vector.tensor_reduce(out=neg_max[:, h : h + 1], in_=s_sb[h][:], axis=AX.X, op=ALU.max, negate=True)
 
         v_codes = sb.tile([P, PACK, P], U32, name="v_codes", align_bytes=64)
         v_scales = sb.tile([P, PACK, P], U8, name="v_scales", align_bytes=64)
 
-        def gather_values(j):
-            g = sb.tile([P, I], F32, name="gathered%d" % j, align_bytes=64)
-            nc.scalar.activation(out=g[:], in_=val_pool[j][:].indirect(offsets[:]), func=ACT.Copy)
+        gathered_tag = ["q_raw1", "page_max1", "gathered2", "gathered3"]
+
+        def gather_values(j, dealt):
+            g = sb.tile([P, I], F32, name="gathered%d" % j, tag=gathered_tag[j], align_bytes=64)
+            window = val_pool[j][:].indirect(offsets[:])
+            if dealt:
+                nc.vector.tensor_copy(out=g[:], in_=window)
+            else:
+                nc.scalar.activation(out=g[:], in_=window, func=ACT.Copy)
             return g
 
-        def centre_values(j, g):
-            sums = sb.tile([P, PAGES], F32, name="sums%d" % j)
-            nc.vector.tensor_reduce(out=sums[:], in_=g[:].rearrange("p (n k) -> p n k", k=PAGE), axis=AX.X, op=ALU.add)
+        def page_sums_vector(j, g, dealt):
+            sums = sb.tile([P, PAGES], F32, name="sums%d" % j, tag="sums%d" % j, align_bytes=64)
+            if dealt:
+                nc.vector.tensor_reduce(
+                    out=sums[:],
+                    in_=g[:].rearrange("p (t n k) -> p n t k", t=PACK, n=PAGES),
+                    axis=AX.XY,
+                    op=ALU.add,
+                )
+            else:
+                nc.vector.tensor_reduce(
+                    out=sums[:], in_=g[:].rearrange("p (n k) -> p n k", k=PAGE), axis=AX.X, op=ALU.add
+                )
+            return sums
+
+        def centre_values(j, g, sums, dealt):
             neg_mean = sb.tile([P, P], F32, name="neg_mean%d" % j, align_bytes=64)
-            nc.gpsimd.tensor_scalar(
-                out=neg_mean[:].rearrange("p (n r) -> p n r", r=PAGE // PACK),
-                in0=sums[:].unsqueeze(2).to_broadcast([P, PAGES, PAGE // PACK]),
-                scalar1=-1.0 / PAGE,
-                scalar2=0.0,
-                op0=ALU.mult,
-                op1=ALU.add,
-            )
+            spread = neg_mean[:].rearrange("p (n r) -> p n r", r=PAGE // PACK)
+            repeated = sums.unsqueeze(2).to_broadcast([P, PAGES, PAGE // PACK])
+            if j == PACK - 1:
+                nc.scalar.activation(out=spread, in_=repeated, func=ACT.Copy, scale=-1.0 / PAGE)
+            else:
+                nc.gpsimd.tensor_scalar(
+                    out=spread, in0=repeated, scalar1=-1.0 / PAGE, scalar2=0.0, op0=ALU.mult, op1=ALU.add
+                )
             turned = ps.tile([P, PACK, P], F32, name="turned", tag="turned", bufs=3)
             for t in range(PACK):
+                place = g[:, t * P : (t + 1) * P] if dealt else g[:, t:I:PACK]
                 nc.tensor.matmul(
-                    turned[:, t, :], lhsT=g[:, t:I:PACK], rhs=ident[:], is_transpose=True, start=(t == 0), stop=False
+                    turned[:, t, :], lhsT=place, rhs=ident[:], is_transpose=True, start=(t == 0), stop=False
                 )
             for t in range(PACK):
                 nc.tensor.matmul(
@@ -174,7 +199,9 @@ def tile_attend_pagelift_lacking_centredvalues_pl_kernel(
             return turned
 
         def scale_values(j, turned):
-            grouped = sb.tile([P, P, PACK], BF16, name="v_grouped%d" % j, align_bytes=64)
+            grouped = sb.tile(
+                [P, P, PACK], BF16, name="v_grouped%d" % j, tag="sums3" if j == 2 else "v_grouped%d" % j, align_bytes=64
+            )
             nc.vector.tensor_tensor(
                 out=grouped[:],
                 in0=turned[:].rearrange("p t e -> p e t"),
@@ -190,26 +217,26 @@ def tile_attend_pagelift_lacking_centredvalues_pl_kernel(
                 in_=grouped[:].rearrange("p e t -> p (e t)"),
             )
 
-        g0 = gather_values(0)
+        g0 = gather_values(0, False)
         for h in range(QT):
-            p = sb.tile([P, I], F32, name="p%d" % h, align_bytes=64)
+            p = sb.tile([P, I], F32, name="p%d" % h, tag="val_pool0" if h == 0 else "p1", align_bytes=64)
             nc.scalar.activation(
                 out=p[:], in_=s_sb[h][:], func=ACT.Exp, bias=neg_max[:, h : h + 1], accum_out=z_sum[:, h : h + 1]
             )
             p_sb.append(p)
-        g1 = gather_values(1)
-        t0 = centre_values(0, g0)
         log_z = sb.tile([P, QT], F32, name="log_z")
         nc.scalar.activation(out=log_z[:], in_=z_sum[:], func=ACT.Ln)
-        t1 = centre_values(1, g1)
+        t0 = centre_values(0, g0, page_sums_vector(0, g0, False)[:], False)
+        g1 = gather_values(1, True)
+        t1 = centre_values(1, g1, page_sums_vector(1, g1, False)[:], False)
         z_res = sb.tile([P, QT], F32, name="z_res")
         nc.vector.tensor_tensor(out=z_res[:], in0=z_sum[:], in1=res_col[:], op=ALU.mult)
         vg0 = scale_values(0, t0)
-        shift = sb.tile([P, QT], F32, name="shift")
+        shift = sb.tile([P, QT], F32, name="shift", tag="sums1", align_bytes=64)
         nc.vector.tensor_tensor(out=shift[:], in0=log_z[:], in1=neg_max[:], op=ALU.subtract)
         quantise_values(0, vg0)
-        g2 = gather_values(2)
-        g3 = gather_values(3)
+        g2 = gather_values(2, False)
+        g3 = gather_values(3, False)
 
         part_sum = sb.tile([P, QT], F32, name="part_sum")
         parts = []
@@ -227,17 +254,16 @@ def tile_attend_pagelift_lacking_centredvalues_pl_kernel(
             parts.append(part)
         neg_den = sb.tile([P, QT], F32, name="neg_den")
         nc.vector.tensor_tensor(out=neg_den[:], in0=part_sum[:], in1=z_res[:], op=ALU.subtract)
-        vg1 = scale_values(1, t1)
+        t2 = centre_values(2, g2, page_sums_vector(2, g2, False)[:], False)
         inv_den = sb.tile([P, QT], F32, name="inv_den")
         nc.vector.reciprocal(out=inv_den[:], in_=neg_den[:])
-        quantise_values(1, vg1)
-        t2 = centre_values(2, g2)
+        vg1 = scale_values(1, t1)
 
         w_codes = sb.tile([P, Q], U32, name="w_codes", align_bytes=64)
         w_scales = sb.tile([P, Q], U8, name="w_scales", align_bytes=64)
-        w_grouped = []
-        for h in range(QT):
-            w = sb.tile([P, I], BF16, name="w%d" % h, align_bytes=64)
+
+        def turn_weights(h):
+            w = sb.tile([P, I], BF16, name="w%d" % h, tag="gathered3" if h == 1 else "w0", align_bytes=64)
             nc.vector.scalar_tensor_tensor(
                 out=w[:].rearrange("q (p t) -> q p t", t=PACK),
                 in0=parts[h][:].rearrange("q (p t) -> q p t", t=PACK),
@@ -250,49 +276,67 @@ def tile_attend_pagelift_lacking_centredvalues_pl_kernel(
             words = w[:].bitcast(F32)
             for u in range(2):
                 nc.tensor.transpose(w_ps[:, u, :], words[:, u : I // 2 : 2], ident[:])
-            grouped = sb.tile([P, P, PACK], BF16, name="w_grouped%d" % h, align_bytes=64)
+            grouped = sb.tile(
+                [P, P, PACK], BF16, name="w_grouped%d" % h, tag="val_pool%d" % (3 - h), align_bytes=64
+            )
             nc.scalar.copy(out=grouped[:].bitcast(F32), in_=w_ps[:].rearrange("p u q -> p q u"))
-            w_grouped.append(grouped)
-        t3 = centre_values(3, g3)
-        vg2 = scale_values(2, t2)
-        for h in range(QT):
+            return grouped
+
+        def quantise_weights(h, grouped):
             nc.vector.quantize_mx(
                 out=w_codes[:, h * P : (h + 1) * P].bitcast(FP8X4),
                 scales=w_scales[:, h * P : (h + 1) * P],
-                in_=w_grouped[h][:].rearrange("p q t -> p (q t)"),
+                in_=grouped[:].rearrange("p q t -> p (q t)"),
             )
+
+        wg0 = turn_weights(0)
+        t3 = centre_values(3, g3, page_sums_vector(3, g3, False)[:], False)
+        wg1 = turn_weights(1)
+        quantise_values(1, vg1)
+        vg2 = scale_values(2, t2)
+        quantise_weights(0, wg0)
         quantise_values(2, vg2)
+        quantise_weights(1, wg1)
         vg3 = scale_values(3, t3)
         quantise_values(3, vg3)
 
-        y = sb.tile([P, PACK, Q], F32, name="y", align_bytes=64)
         out_rows = out_0.rearrange("(p j) q -> p j q", j=PACK)
-        for half in range(2):
-            y_ps = ps.tile([P, 2, Q], F32, name="y_ps", tag="b%d" % half)
-            for r in range(2):
-                j = 2 * half + r
-                nc.tensor.matmul_mx(
-                    out=y_ps[:, r, :],
-                    lhsT=v_codes[:, j, :].bitcast(FP8X4),
-                    lhsT_scale=v_scales[:, j, :],
-                    rhs=w_codes[:].bitcast(FP8X4),
-                    rhs_scale=w_scales[:],
-                    start=True,
-                    stop=True,
-                )
-            nc.scalar.copy(out=y[:, 2 * half : 2 * half + 2, :], in_=y_ps[:])
-            nc.sync.dma_start(out=out_rows[:, 2 * half : 2 * half + 2, :], in_=y[:, 2 * half : 2 * half + 2, :])
+        y_ps = [ps.tile([P, PACK, P], F32, name="y_ps%d" % h, tag="b%d" % h) for h in range(QT)]
+        last = PACK - 1
+        for j, h in [(j, h) for h in range(QT) for j in range(last)] + [(last, h) for h in range(QT)]:
+            cols = slice(h * P, (h + 1) * P)
+            nc.tensor.matmul_mx(
+                out=y_ps[h][:, j, :],
+                lhsT=v_codes[:, j, :].bitcast(FP8X4),
+                lhsT_scale=v_scales[:, j, :],
+                rhs=w_codes[:, cols].bitcast(FP8X4),
+                rhs_scale=w_scales[:, cols],
+                start=True,
+                stop=True,
+            )
 
-        y_grouped = sb.tile([P, Q, PACK], BF16, name="y_grouped", align_bytes=64)
-        nc.vector.tensor_copy(
-            out=y_grouped[:].rearrange("p (c i) j -> p c j i", i=4),
-            in_=y[:].rearrange("p j (c i) -> p c j i", i=4),
-        )
+        def round_result(h):
+            grouped = sb.tile([P, P, PACK], BF16, name="y_grouped%d" % h, align_bytes=64)
+            nc.vector.tensor_copy(out=grouped[:], in_=y_ps[h][:].rearrange("p j q -> p q j"))
+            return grouped
+
+        def store_result(h, queue):
+            y = sb.tile([P, PACK, P], F32, name="y%d" % h, align_bytes=64)
+            nc.scalar.copy(out=y[:], in_=y_ps[h][:])
+            queue.dma_start(out=out_rows[:, :, h * P : (h + 1) * P], in_=y[:])
+
+        y_grouped = [round_result(0)]
+        store_result(1, nc.sync)
+        store_result(0, nc.scalar)
+        y_grouped.append(round_result(1))
         y_codes = sb.tile([P, Q], U32, name="y_codes", align_bytes=64)
         y_scales = sb.tile([P, Q], U8, name="y_scales", align_bytes=64)
-        nc.vector.quantize_mx(
-            out=y_codes[:].bitcast(FP8X4), scales=y_scales[:], in_=y_grouped[:].rearrange("p q j -> p (q j)")
-        )
+        for h in range(QT):
+            nc.vector.quantize_mx(
+                out=y_codes[:, h * P : (h + 1) * P].bitcast(FP8X4),
+                scales=y_scales[:, h * P : (h + 1) * P],
+                in_=y_grouped[h][:].rearrange("p q j -> p (q j)"),
+            )
         nc.sync.dma_start(
             out=out_1[0].rearrange("p q r -> p (q r)").bitcast(I32), in_=y_codes[:].bitcast(I32)
         )

@@ -31,6 +31,7 @@ def tile_attend_pagelift_lacking_centredvalues_pl_kernel(
     nc = tc.nc
     with ExitStack() as ctx:
         sb = ctx.enter_context(tc.tile_pool(name="sb", bufs=1))
+        reuse = ctx.enter_context(tc.tile_pool(name="reuse", bufs=1))
         ps = ctx.enter_context(tc.psum_pool(name="ps", bufs=1))
 
         offsets = sb.tile([P, I // 16], U16, name="offsets")
@@ -59,7 +60,10 @@ def tile_attend_pagelift_lacking_centredvalues_pl_kernel(
         vsc_col = sb.tile([P, PACK], F32, name="vsc_col")
 
         def load_values(j):
-            pool_j = sb.tile([P, T], F32, name="val_pool%d" % j, tag="val_pool%d" % j, align_bytes=64)
+            if j == 1:
+                pool_j = reuse.tile([P, T], F32, name="val_pool1", align_bytes=64, offset=0)
+            else:
+                pool_j = sb.tile([P, T], F32, name="val_pool%d" % j, tag="val_pool%d" % j, align_bytes=64)
             nc.sync.dma_start(out=pool_j[:], in_=vals.rearrange("(p j) t -> j p t", j=PACK)[j])
             return pool_j
 
@@ -138,43 +142,44 @@ def tile_attend_pagelift_lacking_centredvalues_pl_kernel(
                 op1=ALU.add,
             )
             s_sb.append(s)
-        neg_max = sb.tile([P, QT], F32, name="neg_max", tag="gathered3", align_bytes=64)
+        neg_max = sb.tile([P, QT], F32, name="neg_max")
         for h in range(QT):
             nc.vector.tensor_reduce(out=neg_max[:, h : h + 1], in_=s_sb[h][:], axis=AX.X, op=ALU.max, negate=True)
 
         v_codes = sb.tile([P, PACK, P], U32, name="v_codes", align_bytes=64)
         v_scales = sb.tile([P, PACK, P], U8, name="v_scales", align_bytes=64)
 
-        gathered_tag = ["q_raw1", "page_max1", "gathered2", "gathered3"]
+        gathered_tag = ["q_raw1", "page_max1", "gathered2", "val_pool2"]
 
-        def gather_values(j, dealt):
+        def gather_values(j):
             g = sb.tile([P, I], F32, name="gathered%d" % j, tag=gathered_tag[j], align_bytes=64)
             window = val_pool[j][:].indirect(offsets[:])
-            if dealt:
+            if j == 1:
                 nc.vector.tensor_copy(out=g[:], in_=window)
             else:
                 nc.scalar.activation(out=g[:], in_=window, func=ACT.Copy)
-            return g
-
-        def page_sums_vector(j, g, dealt):
-            sums = sb.tile([P, PAGES], F32, name="sums%d" % j, tag="sums%d" % j, align_bytes=64)
-            if dealt:
-                nc.vector.tensor_reduce(
-                    out=sums[:],
-                    in_=g[:].rearrange("p (t n k) -> p n t k", t=PACK, n=PAGES),
-                    axis=AX.XY,
-                    op=ALU.add,
+            dealt = sb.tile([P, PACK, P], F32, name="dealt%d" % j, align_bytes=64)
+            if j == 1:
+                nc.gpsimd.tensor_scalar(
+                    out=dealt[:].rearrange("e t (c i) -> e c t i", i=4),
+                    in0=g[:].rearrange("e (c i t) -> e c t i", i=4, t=PACK),
+                    scalar1=1.0,
+                    scalar2=0.0,
+                    op0=ALU.mult,
+                    op1=ALU.add,
                 )
             else:
-                nc.vector.tensor_reduce(
-                    out=sums[:], in_=g[:].rearrange("p (n k) -> p n k", k=PAGE), axis=AX.X, op=ALU.add
+                nc.scalar.copy(
+                    out=dealt[:].rearrange("e t p -> e p t"), in_=g[:].rearrange("e (p t) -> e p t", t=PACK)
                 )
-            return sums
+            return g, dealt
 
-        def centre_values(j, g, sums, dealt):
+        def centre_values(j, g, dealt):
+            sums = sb.tile([P, PAGES], F32, name="sums%d" % j, tag="sums%d" % j, align_bytes=64)
+            nc.vector.tensor_reduce(out=sums[:], in_=g[:].rearrange("p (n k) -> p n k", k=PAGE), axis=AX.X, op=ALU.add)
             neg_mean = sb.tile([P, P], F32, name="neg_mean%d" % j, align_bytes=64)
             spread = neg_mean[:].rearrange("p (n r) -> p n r", r=PAGE // PACK)
-            repeated = sums.unsqueeze(2).to_broadcast([P, PAGES, PAGE // PACK])
+            repeated = sums[:].unsqueeze(2).to_broadcast([P, PAGES, PAGE // PACK])
             if j == PACK - 1:
                 nc.scalar.activation(out=spread, in_=repeated, func=ACT.Copy, scale=-1.0 / PAGE)
             else:
@@ -183,9 +188,8 @@ def tile_attend_pagelift_lacking_centredvalues_pl_kernel(
                 )
             turned = ps.tile([P, PACK, P], F32, name="turned", tag="turned", bufs=3)
             for t in range(PACK):
-                place = g[:, t * P : (t + 1) * P] if dealt else g[:, t:I:PACK]
                 nc.tensor.matmul(
-                    turned[:, t, :], lhsT=place, rhs=ident[:], is_transpose=True, start=(t == 0), stop=False
+                    turned[:, t, :], lhsT=dealt[:, t, :], rhs=ident[:], is_transpose=True, start=(t == 0), stop=False
                 )
             for t in range(PACK):
                 nc.tensor.matmul(
@@ -199,9 +203,16 @@ def tile_attend_pagelift_lacking_centredvalues_pl_kernel(
             return turned
 
         def scale_values(j, turned):
-            grouped = sb.tile(
-                [P, P, PACK], BF16, name="v_grouped%d" % j, tag="sums3" if j == 2 else "v_grouped%d" % j, align_bytes=64
-            )
+            if j == 0:
+                grouped = reuse.tile([P, P, PACK], BF16, name="v_grouped0", align_bytes=64, offset=0)
+            else:
+                grouped = sb.tile(
+                    [P, P, PACK],
+                    BF16,
+                    name="v_grouped%d" % j,
+                    tag="sums3" if j == 2 else "v_grouped%d" % j,
+                    align_bytes=64,
+                )
             nc.vector.tensor_tensor(
                 out=grouped[:],
                 in0=turned[:].rearrange("p t e -> p e t"),
@@ -217,7 +228,7 @@ def tile_attend_pagelift_lacking_centredvalues_pl_kernel(
                 in_=grouped[:].rearrange("p e t -> p (e t)"),
             )
 
-        g0 = gather_values(0, False)
+        g0 = gather_values(0)
         for h in range(QT):
             p = sb.tile([P, I], F32, name="p%d" % h, tag="val_pool0" if h == 0 else "p1", align_bytes=64)
             nc.scalar.activation(
@@ -226,17 +237,17 @@ def tile_attend_pagelift_lacking_centredvalues_pl_kernel(
             p_sb.append(p)
         log_z = sb.tile([P, QT], F32, name="log_z")
         nc.scalar.activation(out=log_z[:], in_=z_sum[:], func=ACT.Ln)
-        t0 = centre_values(0, g0, page_sums_vector(0, g0, False)[:], False)
-        g1 = gather_values(1, True)
-        t1 = centre_values(1, g1, page_sums_vector(1, g1, False)[:], False)
-        z_res = sb.tile([P, QT], F32, name="z_res")
-        nc.vector.tensor_tensor(out=z_res[:], in0=z_sum[:], in1=res_col[:], op=ALU.mult)
+        t0 = centre_values(0, *g0)
+        g1 = gather_values(1)
+        t1 = centre_values(1, *g1)
         vg0 = scale_values(0, t0)
-        shift = sb.tile([P, QT], F32, name="shift", tag="sums1", align_bytes=64)
+        z_res = sb.tile([P, QT], F32, name="z_res")
+        nc.gpsimd.tensor_tensor(out=z_res[:], in0=z_sum[:], in1=res_col[:], op=ALU.mult)
+        shift = reuse.tile([P, QT], F32, name="shift", align_bytes=64, offset=1024)
         nc.vector.tensor_tensor(out=shift[:], in0=log_z[:], in1=neg_max[:], op=ALU.subtract)
         quantise_values(0, vg0)
-        g2 = gather_values(2, False)
-        g3 = gather_values(3, False)
+        g2 = gather_values(2)
+        g3 = gather_values(3)
 
         part_sum = sb.tile([P, QT], F32, name="part_sum")
         parts = []
@@ -254,7 +265,7 @@ def tile_attend_pagelift_lacking_centredvalues_pl_kernel(
             parts.append(part)
         neg_den = sb.tile([P, QT], F32, name="neg_den")
         nc.vector.tensor_tensor(out=neg_den[:], in0=part_sum[:], in1=z_res[:], op=ALU.subtract)
-        t2 = centre_values(2, g2, page_sums_vector(2, g2, False)[:], False)
+        t2 = centre_values(2, *g2)
         inv_den = sb.tile([P, QT], F32, name="inv_den")
         nc.vector.reciprocal(out=inv_den[:], in_=neg_den[:])
         vg1 = scale_values(1, t1)
@@ -263,7 +274,7 @@ def tile_attend_pagelift_lacking_centredvalues_pl_kernel(
         w_scales = sb.tile([P, Q], U8, name="w_scales", align_bytes=64)
 
         def turn_weights(h):
-            w = sb.tile([P, I], BF16, name="w%d" % h, tag="gathered3" if h == 1 else "w0", align_bytes=64)
+            w = sb.tile([P, I], BF16, name="w%d" % h, tag="val_pool2" if h == 1 else "w0", align_bytes=64)
             nc.vector.scalar_tensor_tensor(
                 out=w[:].rearrange("q (p t) -> q p t", t=PACK),
                 in0=parts[h][:].rearrange("q (p t) -> q p t", t=PACK),
@@ -277,7 +288,7 @@ def tile_attend_pagelift_lacking_centredvalues_pl_kernel(
             for u in range(2):
                 nc.tensor.transpose(w_ps[:, u, :], words[:, u : I // 2 : 2], ident[:])
             grouped = sb.tile(
-                [P, P, PACK], BF16, name="w_grouped%d" % h, tag="val_pool%d" % (3 - h), align_bytes=64
+                [P, P, PACK], BF16, name="w_grouped%d" % h, tag="val_pool3" if h == 0 else "w_grouped1", align_bytes=64
             )
             nc.scalar.copy(out=grouped[:].bitcast(F32), in_=w_ps[:].rearrange("p u q -> p q u"))
             return grouped
@@ -290,7 +301,7 @@ def tile_attend_pagelift_lacking_centredvalues_pl_kernel(
             )
 
         wg0 = turn_weights(0)
-        t3 = centre_values(3, g3, page_sums_vector(3, g3, False)[:], False)
+        t3 = centre_values(3, *g3)
         wg1 = turn_weights(1)
         quantise_values(1, vg1)
         vg2 = scale_values(2, t2)

@@ -60,8 +60,8 @@ def tile_attend_pagelift_lacking_centredvalues_pl_kernel(
         vsc_col = sb.tile([P, PACK], F32, name="vsc_col")
 
         def load_values(j):
-            if j == 1:
-                pool_j = reuse.tile([P, T], F32, name="val_pool1", align_bytes=64, offset=0)
+            if j % 2 == 1:
+                pool_j = reuse.tile([P, T], F32, name="val_pool%d" % j, align_bytes=64, offset=8192 * (j - 1))
             else:
                 pool_j = sb.tile([P, T], F32, name="val_pool%d" % j, tag="val_pool%d" % j, align_bytes=64)
             nc.sync.dma_start(out=pool_j[:], in_=vals.rearrange("(p j) t -> j p t", j=PACK)[j])
@@ -69,12 +69,12 @@ def tile_attend_pagelift_lacking_centredvalues_pl_kernel(
 
         with nc.allow_non_contiguous_dma(reason="one value a partition"):
             nc.sync.dma_start(out=lam_col[:], in_=lam.rearrange("(h p) o -> p (h o)", p=P))
-        val_pool = [load_values(0)]
+        val_pool = [load_values(0), load_values(1)]
         nc.sync.dma_start(out=vsc_col[:], in_=vsc.rearrange("o (p t) -> p (o t)", t=PACK))
         nc.sync.dma_start(out=os_col[:], in_=os_row.rearrange("o (p t) -> p (o t)", t=PACK))
         with nc.allow_non_contiguous_dma(reason="one value a partition"):
             nc.sync.dma_start(out=res_col[:], in_=reserve.rearrange("(h p) o -> p (h o)", p=P))
-        val_pool.extend(load_values(j) for j in range(1, PACK))
+        val_pool.extend(load_values(j) for j in range(2, PACK))
 
         ident = sb.tile([P, P], F32, name="ident", align_bytes=64)
         make_identity(nc, ident[:])
@@ -119,12 +119,12 @@ def tile_attend_pagelift_lacking_centredvalues_pl_kernel(
         b_ps = [score(0, h, "b%d" % h) for h in range(QT)]
         a_ps = [score(1, h, "a%d" % h) for h in range(QT)]
 
-        os_ps = ps.tile([P, PACK, P], F32, name="os_ps")
+        os_ps = ps.tile([P, PACK, P], F32, name="os_ps", tag="os_ps")
         for t in range(PACK):
             nc.tensor.transpose(os_ps[:, t, :], os_col[:, t : t + 1].to_broadcast([P, P]), ident[:])
 
         page_max, s_sb, p_sb, neg_max = [], [], [], []
-        z_sum = sb.tile([P, QT], F32, name="z_sum", tag="gathered2", align_bytes=64)
+        z_sum = sb.tile([P, QT], F32, name="z_sum")
         for h in range(QT):
             mb = sb.tile([P, PAGES], F32, name="page_max%d" % h, tag="page_max%d" % h, align_bytes=64)
             nc.vector.tensor_reduce(
@@ -152,7 +152,10 @@ def tile_attend_pagelift_lacking_centredvalues_pl_kernel(
         gathered_tag = ["q_raw1", "page_max1", "gathered2", "val_pool2"]
 
         def gather_values(j):
-            g = sb.tile([P, I], F32, name="gathered%d" % j, tag=gathered_tag[j], align_bytes=64)
+            if j == 2:
+                g = reuse.tile([P, I], F32, name="gathered2", align_bytes=64, offset=8192)
+            else:
+                g = sb.tile([P, I], F32, name="gathered%d" % j, tag=gathered_tag[j], align_bytes=64)
             window = val_pool[j][:].indirect(offsets[:])
             if j == 1:
                 nc.vector.tensor_copy(out=g[:], in_=window)
@@ -210,7 +213,7 @@ def tile_attend_pagelift_lacking_centredvalues_pl_kernel(
                     [P, P, PACK],
                     BF16,
                     name="v_grouped%d" % j,
-                    tag="sums3" if j == 2 else "v_grouped%d" % j,
+                    tag=("", "val_pool2", "sums3", "v_grouped3")[j],
                     align_bytes=64,
                 )
             nc.vector.tensor_tensor(
@@ -235,7 +238,7 @@ def tile_attend_pagelift_lacking_centredvalues_pl_kernel(
                 out=p[:], in_=s_sb[h][:], func=ACT.Exp, bias=neg_max[:, h : h + 1], accum_out=z_sum[:, h : h + 1]
             )
             p_sb.append(p)
-        log_z = sb.tile([P, QT], F32, name="log_z")
+        log_z = reuse.tile([P, QT], F32, name="log_z", align_bytes=64, offset=8192)
         nc.scalar.activation(out=log_z[:], in_=z_sum[:], func=ACT.Ln)
         t0 = centre_values(0, *g0)
         g1 = gather_values(1)
@@ -244,7 +247,14 @@ def tile_attend_pagelift_lacking_centredvalues_pl_kernel(
         z_res = sb.tile([P, QT], F32, name="z_res")
         nc.gpsimd.tensor_tensor(out=z_res[:], in0=z_sum[:], in1=res_col[:], op=ALU.mult)
         shift = reuse.tile([P, QT], F32, name="shift", align_bytes=64, offset=1024)
-        nc.vector.tensor_tensor(out=shift[:], in0=log_z[:], in1=neg_max[:], op=ALU.subtract)
+        for h in range(QT):
+            nc.scalar.activation(
+                out=shift[:, h : h + 1],
+                in_=log_z[:, h : h + 1],
+                func=ACT.Identity,
+                scale=-1.0,
+                bias=neg_max[:, h : h + 1],
+            )
         quantise_values(0, vg0)
         g2 = gather_values(2)
         g3 = gather_values(3)
@@ -258,23 +268,22 @@ def tile_attend_pagelift_lacking_centredvalues_pl_kernel(
                 in0=s_sb[h][:],
                 scalar=shift[:, h : h + 1],
                 in1=p_sb[h][:],
-                op0=ALU.subtract,
+                op0=ALU.add,
                 op1=ALU.mult,
                 accum_out=part_sum[:, h : h + 1],
             )
             parts.append(part)
         neg_den = sb.tile([P, QT], F32, name="neg_den")
-        nc.vector.tensor_tensor(out=neg_den[:], in0=part_sum[:], in1=z_res[:], op=ALU.subtract)
+        nc.gpsimd.tensor_tensor(out=neg_den[:], in0=part_sum[:], in1=z_res[:], op=ALU.subtract)
         t2 = centre_values(2, *g2)
-        inv_den = sb.tile([P, QT], F32, name="inv_den")
+        inv_den = reuse.tile([P, QT], F32, name="inv_den", align_bytes=64, offset=8192 + 1024)
         nc.vector.reciprocal(out=inv_den[:], in_=neg_den[:])
-        vg1 = scale_values(1, t1)
 
         w_codes = sb.tile([P, Q], U32, name="w_codes", align_bytes=64)
         w_scales = sb.tile([P, Q], U8, name="w_scales", align_bytes=64)
 
         def turn_weights(h):
-            w = sb.tile([P, I], BF16, name="w%d" % h, tag="val_pool2" if h == 1 else "w0", align_bytes=64)
+            w = sb.tile([P, I], BF16, name="w%d" % h, align_bytes=64)
             nc.vector.scalar_tensor_tensor(
                 out=w[:].rearrange("q (p t) -> q p t", t=PACK),
                 in0=parts[h][:].rearrange("q (p t) -> q p t", t=PACK),
@@ -287,9 +296,10 @@ def tile_attend_pagelift_lacking_centredvalues_pl_kernel(
             words = w[:].bitcast(F32)
             for u in range(2):
                 nc.tensor.transpose(w_ps[:, u, :], words[:, u : I // 2 : 2], ident[:])
-            grouped = sb.tile(
-                [P, P, PACK], BF16, name="w_grouped%d" % h, tag="val_pool3" if h == 0 else "w_grouped1", align_bytes=64
-            )
+            if h == 0:
+                grouped = reuse.tile([P, P, PACK], BF16, name="w_grouped0", align_bytes=64, offset=16384)
+            else:
+                grouped = sb.tile([P, P, PACK], BF16, name="w_grouped1", align_bytes=64)
             nc.scalar.copy(out=grouped[:].bitcast(F32), in_=w_ps[:].rearrange("p u q -> p q u"))
             return grouped
 
@@ -301,23 +311,22 @@ def tile_attend_pagelift_lacking_centredvalues_pl_kernel(
             )
 
         wg0 = turn_weights(0)
-        t3 = centre_values(3, *g3)
         wg1 = turn_weights(1)
+        t3 = centre_values(3, *g3)
+        vg1 = scale_values(1, t1)
+        quantise_weights(0, wg0)
+        quantise_weights(1, wg1)
         quantise_values(1, vg1)
         vg2 = scale_values(2, t2)
-        quantise_weights(0, wg0)
-        quantise_values(2, vg2)
-        quantise_weights(1, wg1)
         vg3 = scale_values(3, t3)
+        quantise_values(2, vg2)
         quantise_values(3, vg3)
 
         out_rows = out_0.rearrange("(p j) q -> p j q", j=PACK)
-        y_ps = [ps.tile([P, PACK, P], F32, name="y_ps%d" % h, tag="b%d" % h) for h in range(QT)]
-        last = PACK - 1
-        for j, h in [(j, h) for h in range(QT) for j in range(last)] + [(last, h) for h in range(QT)]:
-            cols = slice(h * P, (h + 1) * P)
+
+        def product(out, j, cols):
             nc.tensor.matmul_mx(
-                out=y_ps[h][:, j, :],
+                out=out,
                 lhsT=v_codes[:, j, :].bitcast(FP8X4),
                 lhsT_scale=v_scales[:, j, :],
                 rhs=w_codes[:, cols].bitcast(FP8X4),
@@ -326,26 +335,30 @@ def tile_attend_pagelift_lacking_centredvalues_pl_kernel(
                 stop=True,
             )
 
-        def round_result(h):
-            grouped = sb.tile([P, P, PACK], BF16, name="y_grouped%d" % h, align_bytes=64)
-            nc.vector.tensor_copy(out=grouped[:], in_=y_ps[h][:].rearrange("p j q -> p q j"))
-            return grouped
+        halves = [slice(h * P, (h + 1) * P) for h in range(QT)]
+        y_ps = [ps.tile([P, PACK, P], F32, name="y_ps%d" % h, tag="b%d" % h) for h in range(QT)]
+        y_pair = [sb.tile([P, 2, Q], F32, name="y_pair%d" % n, align_bytes=64) for n in range(2)]
+        for h in range(QT):
+            for j in range(2):
+                product(y_ps[h][:, j, :], j, halves[h])
+            nc.scalar.copy(out=y_pair[0][:, :, halves[h]], in_=y_ps[h][:, 0:2, :])
+        nc.sync.dma_start(out=out_rows[:, 0:2, :], in_=y_pair[0][:])
+        for j in range(2, PACK):
+            for h in range(QT):
+                product(y_ps[h][:, j, :], j, halves[h])
 
-        def store_result(h, queue):
-            y = sb.tile([P, PACK, P], F32, name="y%d" % h, align_bytes=64)
-            nc.scalar.copy(out=y[:], in_=y_ps[h][:])
-            queue.dma_start(out=out_rows[:, :, h * P : (h + 1) * P], in_=y[:])
-
-        y_grouped = [round_result(0)]
-        store_result(1, nc.sync)
-        store_result(0, nc.scalar)
-        y_grouped.append(round_result(1))
+        y_grouped = [sb.tile([P, P, PACK], BF16, name="y_grouped%d" % h, align_bytes=64) for h in range(QT)]
+        nc.vector.tensor_copy(out=y_grouped[0][:], in_=y_ps[0][:].rearrange("p j q -> p q j"))
+        nc.scalar.copy(out=y_grouped[1][:], in_=y_ps[1][:].rearrange("p j q -> p q j"))
+        for h in range(QT):
+            nc.scalar.copy(out=y_pair[1][:, :, halves[h]], in_=y_ps[h][:, 2:PACK, :])
+        nc.scalar.dma_start(out=out_rows[:, 2:PACK, :], in_=y_pair[1][:])
         y_codes = sb.tile([P, Q], U32, name="y_codes", align_bytes=64)
         y_scales = sb.tile([P, Q], U8, name="y_scales", align_bytes=64)
         for h in range(QT):
             nc.vector.quantize_mx(
-                out=y_codes[:, h * P : (h + 1) * P].bitcast(FP8X4),
-                scales=y_scales[:, h * P : (h + 1) * P],
+                out=y_codes[:, halves[h]].bitcast(FP8X4),
+                scales=y_scales[:, halves[h]],
                 in_=y_grouped[h][:].rearrange("p q j -> p (q j)"),
             )
         nc.sync.dma_start(

from contextlib import ExitStack

import concourse.mybir as mybir
from concourse.masks import make_identity

D, T, I, Q, E = 512, 2048, 512, 256, 512
P = 128
PACK = 4
PAGE = 16
PAGES = I // PAGE
QT = Q // P

F32 = mybir.dt.float32
BF16 = mybir.dt.bfloat16
I32 = mybir.dt.int32
U32 = mybir.dt.uint32
U16 = mybir.dt.uint16
U8 = mybir.dt.uint8
FP8X4 = mybir.dt.float8_e4m3fn_x4
FP4X4 = mybir.dt.float4_e2m1fn_x4
ALU = mybir.AluOpType
ACT = mybir.ActivationFunctionType
AX = mybir.AxisListType

FLOPS = 2 * 2 * D * Q * I + 2 * I * E * Q


def tile_attend_pagelift_lacking_centredvalues_pl_kernel(
    tc, query, query2, keys_words, keys_scales, lam, reserve, os_row, vals, vsc, offs, out_0, out_1, out_2
):
    nc = tc.nc
    with ExitStack() as ctx:
        sb = ctx.enter_context(tc.tile_pool(name="sb", bufs=1))
        reuse = ctx.enter_context(tc.tile_pool(name="reuse", bufs=1))
        ps = ctx.enter_context(tc.psum_pool(name="ps", bufs=1))

        offsets = sb.tile([P, I // 16], U16, name="offsets")
        nc.sync.dma_start(offsets[:], offs)

        key_words = sb.tile([P, T], U16, name="key_words", align_bytes=64)
        nc.sync.dma_start(out=key_words[:].bitcast(I32), in_=keys_words[0].bitcast(I32))

        key_scales = sb.tile([P, T], U8, name="key_scales", align_bytes=64)
        nc.gpsimd.memset(key_scales[:].bitcast(I32), 0)
        for quad in range(4):
            nc.sync.dma_start(
                out=key_scales[32 * quad : 32 * quad + 4, :].bitcast(I32),
                in_=keys_scales[0, 4 * quad : 4 * quad + 4, :].bitcast(I32),
            )

        q_raw = []
        for n, src in enumerate((query2, query)):
            raw = sb.tile([P, PACK, Q], F32, name="q_raw%d" % n, tag="q_raw%d" % n, align_bytes=64)
            nc.sync.dma_start(out=raw[:], in_=src.rearrange("(p t) q -> p t q", t=PACK))
            q_raw.append(raw)

        lam_col = sb.tile([P, QT], F32, name="lam_col")
        res_col = sb.tile([P, QT], F32, name="res_col")
        os_col = sb.tile([P, PACK], F32, name="os_col")
        vsc_col = sb.tile([P, PACK], F32, name="vsc_col")

        def load_values(j):
            if j % 2 == 1:
                pool_j = reuse.tile([P, T], F32, name="val_pool%d" % j, align_bytes=64, offset=8192 * (j - 1))
            else:
                pool_j = sb.tile([P, T], F32, name="val_pool%d" % j, tag="val_pool%d" % j, align_bytes=64)
            nc.sync.dma_start(out=pool_j[:], in_=vals.rearrange("(p j) t -> j p t", j=PACK)[j])
            return pool_j

        with nc.allow_non_contiguous_dma(reason="one value a partition"):
            nc.sync.dma_start(out=lam_col[:], in_=lam.rearrange("(h p) o -> p (h o)", p=P))
        val_pool = [load_values(0), load_values(1)]
        nc.sync.dma_start(out=vsc_col[:], in_=vsc.rearrange("o (p t) -> p (o t)", t=PACK))
        nc.sync.dma_start(out=os_col[:], in_=os_row.rearrange("o (p t) -> p (o t)", t=PACK))
        with nc.allow_non_contiguous_dma(reason="one value a partition"):
            nc.sync.dma_start(out=res_col[:], in_=reserve.rearrange("(h p) o -> p (h o)", p=P))
        val_pool.extend(load_values(j) for j in range(2, PACK))

        ident = sb.tile([P, P], F32, name="ident", align_bytes=64)
        make_identity(nc, ident[:])

        kg_words = sb.tile([P, I], U16, name="kg_words", align_bytes=64)
        kg_scales = sb.tile([P, I], U8, name="kg_scales", align_bytes=64)
        nc.vector.tensor_copy(kg_words[:], key_words[:].indirect(offsets[:]))
        nc.vector.tensor_copy(kg_scales[:], key_scales[:].indirect(offsets[:]))

        q_codes, q_scales = [], []
        for n in range(2):
            codes = sb.tile([P, Q], U32, name="q_codes%d" % n, align_bytes=64)
            scales = sb.tile([P, Q], U8, name="q_scales%d" % n, align_bytes=64)
            for h in range(QT):
                cols = slice(h * P, (h + 1) * P)
                grouped = sb.tile([P, P, PACK], BF16, name="q_grouped%d%d" % (n, h), align_bytes=64)
                dst = grouped[:].rearrange("p (c i) t -> p c t i", i=4)
                src = q_raw[n][:, :, cols].rearrange("p t (c i) -> p c t i", i=4)
                nc.scalar.activation(out=dst, in_=src, func=ACT.Copy)
                nc.vector.quantize_mx(
                    out=codes[:, cols].bitcast(FP8X4),
                    scales=scales[:, cols],
                    in_=grouped[:].rearrange("p q t -> p (q t)"),
                )
            q_codes.append(codes)
            q_scales.append(scales)

        def score(n, h, tag):
            bank = ps.tile([P, I], F32, name="score", tag=tag)
            cols = slice(h * P, (h + 1) * P)
            nc.tensor.matmul_mx(
                out=bank[:],
                lhsT=q_codes[n][:, cols].bitcast(FP8X4),
                lhsT_scale=q_scales[n][:, cols],
                rhs=kg_words[:].bitcast(FP4X4),
                rhs_scale=kg_scales[:],
                start=True,
                stop=True,
            )
            return bank

        b_ps = [score(0, h, "b%d" % h) for h in range(QT)]
        a_ps = [score(1, h, "a%d" % h) for h in range(QT)]

        os_ps = ps.tile([P, PACK, P], F32, name="os_ps", tag="os_ps")
        for t in range(PACK):
            nc.tensor.transpose(os_ps[:, t, :], os_col[:, t : t + 1].to_broadcast([P, P]), ident[:])

        page_max, s_sb, p_sb, neg_max = [], [], [], []
        z_sum = sb.tile([P, QT], F32, name="z_sum")
        for h in range(QT):
            mb = sb.tile([P, PAGES], F32, name="page_max%d" % h, tag="page_max%d" % h, align_bytes=64)
            nc.vector.tensor_reduce(
                out=mb[:], in_=b_ps[h][:].rearrange("p (n k) -> p n k", k=PAGE), axis=AX.X, op=ALU.max
            )
            page_max.append(mb)
        for h in range(QT):
            s = sb.tile([P, I], F32, name="s%d" % h, align_bytes=64)
            nc.vector.scalar_tensor_tensor(
                out=s[:].rearrange("p (n k) -> p n k", k=PAGE),
                in0=page_max[h][:].unsqueeze(2).to_broadcast([P, PAGES, PAGE]),
                scalar=lam_col[:, h : h + 1],
                in1=a_ps[h][:].rearrange("p (n k) -> p n k", k=PAGE),
                op0=ALU.mult,
                op1=ALU.add,
            )
            s_sb.append(s)
        neg_max = sb.tile([P, QT], F32, name="neg_max")
        for h in range(QT):
            nc.vector.tensor_reduce(out=neg_max[:, h : h + 1], in_=s_sb[h][:], axis=AX.X, op=ALU.max, negate=True)

        v_codes = sb.tile([P, PACK, P], U32, name="v_codes", align_bytes=64)
        v_scales = sb.tile([P, PACK, P], U8, name="v_scales", align_bytes=64)

        gathered_tag = ["q_raw1", "page_max1", "gathered2", "val_pool2"]

        def gather_values(j):
            if j == 2:
                g = reuse.tile([P, I], F32, name="gathered2", align_bytes=64, offset=8192)
            else:
                g = sb.tile([P, I], F32, name="gathered%d" % j, tag=gathered_tag[j], align_bytes=64)
            window = val_pool[j][:].indirect(offsets[:])
            if j == 1:
                nc.vector.tensor_copy(out=g[:], in_=window)
            else:
                nc.scalar.activation(out=g[:], in_=window, func=ACT.Copy)
            dealt = sb.tile([P, PACK, P], F32, name="dealt%d" % j, align_bytes=64)
            if j == 1:
                nc.gpsimd.tensor_scalar(
                    out=dealt[:].rearrange("e t (c i) -> e c t i", i=4),
                    in0=g[:].rearrange("e (c i t) -> e c t i", i=4, t=PACK),
                    scalar1=1.0,
                    scalar2=0.0,
                    op0=ALU.mult,
                    op1=ALU.add,
                )
            else:
                nc.scalar.copy(
                    out=dealt[:].rearrange("e t p -> e p t"), in_=g[:].rearrange("e (p t) -> e p t", t=PACK)
                )
            return g, dealt

        def centre_values(j, g, dealt):
            sums = sb.tile([P, PAGES], F32, name="sums%d" % j, tag="sums%d" % j, align_bytes=64)
            nc.vector.tensor_reduce(out=sums[:], in_=g[:].rearrange("p (n k) -> p n k", k=PAGE), axis=AX.X, op=ALU.add)
            neg_mean = sb.tile([P, P], F32, name="neg_mean%d" % j, align_bytes=64)
            spread = neg_mean[:].rearrange("p (n r) -> p n r", r=PAGE // PACK)
            repeated = sums[:].unsqueeze(2).to_broadcast([P, PAGES, PAGE // PACK])
            if j == PACK - 1:
                nc.scalar.activation(out=spread, in_=repeated, func=ACT.Copy, scale=-1.0 / PAGE)
            else:
                nc.gpsimd.tensor_scalar(
                    out=spread, in0=repeated, scalar1=-1.0 / PAGE, scalar2=0.0, op0=ALU.mult, op1=ALU.add
                )
            turned = ps.tile([P, PACK, P], F32, name="turned", tag="turned", bufs=3)
            for t in range(PACK):
                nc.tensor.matmul(
                    turned[:, t, :], lhsT=dealt[:, t, :], rhs=ident[:], is_transpose=True, start=(t == 0), stop=False
                )
            for t in range(PACK):
                nc.tensor.matmul(
                    turned[:, t, :],
                    lhsT=neg_mean[:],
                    rhs=ident[:],
                    is_transpose=True,
                    start=False,
                    stop=(t == PACK - 1),
                )
            return turned

        def scale_values(j, turned):
            if j == 0:
                grouped = reuse.tile([P, P, PACK], BF16, name="v_grouped0", align_bytes=64, offset=0)
            else:
                grouped = sb.tile(
                    [P, P, PACK],
                    BF16,
                    name="v_grouped%d" % j,
                    tag=("", "val_pool2", "sums3", "v_grouped3")[j],
                    align_bytes=64,
                )
            nc.vector.tensor_tensor(
                out=grouped[:],
                in0=turned[:].rearrange("p t e -> p e t"),
                in1=vsc_col[:].unsqueeze(1).to_broadcast([P, P, PACK]),
                op=ALU.mult,
            )
            return grouped

        def quantise_values(j, grouped):
            nc.vector.quantize_mx(
                out=v_codes[:, j, :].bitcast(FP8X4),
                scales=v_scales[:, j, :],
                in_=grouped[:].rearrange("p e t -> p (e t)"),
            )

        g0 = gather_values(0)
        for h in range(QT):
            p = sb.tile([P, I], F32, name="p%d" % h, tag="val_pool0" if h == 0 else "p1", align_bytes=64)
            nc.scalar.activation(
                out=p[:], in_=s_sb[h][:], func=ACT.Exp, bias=neg_max[:, h : h + 1], accum_out=z_sum[:, h : h + 1]
            )
            p_sb.append(p)
        log_z = reuse.tile([P, QT], F32, name="log_z", align_bytes=64, offset=8192)
        nc.scalar.activation(out=log_z[:], in_=z_sum[:], func=ACT.Ln)
        t0 = centre_values(0, *g0)
        g1 = gather_values(1)
        t1 = centre_values(1, *g1)
        vg0 = scale_values(0, t0)
        z_res = sb.tile([P, QT], F32, name="z_res")
        nc.gpsimd.tensor_tensor(out=z_res[:], in0=z_sum[:], in1=res_col[:], op=ALU.mult)
        shift = reuse.tile([P, QT], F32, name="shift", align_bytes=64, offset=1024)
        for h in range(QT):
            nc.scalar.activation(
                out=shift[:, h : h + 1],
                in_=log_z[:, h : h + 1],
                func=ACT.Identity,
                scale=-1.0,
                bias=neg_max[:, h : h + 1],
            )
        quantise_values(0, vg0)
        g2 = gather_values(2)
        g3 = gather_values(3)

        part_sum = sb.tile([P, QT], F32, name="part_sum")
        parts = []
        for h in range(QT):
            part = sb.tile([P, I], F32, name="part%d" % h, align_bytes=64)
            nc.vector.scalar_tensor_tensor(
                out=part[:],
                in0=s_sb[h][:],
                scalar=shift[:, h : h + 1],
                in1=p_sb[h][:],
                op0=ALU.add,
                op1=ALU.mult,
                accum_out=part_sum[:, h : h + 1],
            )
            parts.append(part)
        neg_den = sb.tile([P, QT], F32, name="neg_den")
        nc.gpsimd.tensor_tensor(out=neg_den[:], in0=part_sum[:], in1=z_res[:], op=ALU.subtract)
        t2 = centre_values(2, *g2)
        inv_den = reuse.tile([P, QT], F32, name="inv_den", align_bytes=64, offset=8192 + 1024)
        nc.vector.reciprocal(out=inv_den[:], in_=neg_den[:])

        w_codes = sb.tile([P, Q], U32, name="w_codes", align_bytes=64)
        w_scales = sb.tile([P, Q], U8, name="w_scales", align_bytes=64)

        def turn_weights(h):
            w = sb.tile([P, I], BF16, name="w%d" % h, align_bytes=64)
            nc.vector.scalar_tensor_tensor(
                out=w[:].rearrange("q (p t) -> q p t", t=PACK),
                in0=parts[h][:].rearrange("q (p t) -> q p t", t=PACK),
                scalar=inv_den[:, h : h + 1],
                in1=os_ps[:].rearrange("q t p -> q p t"),
                op0=ALU.mult,
                op1=ALU.mult,
            )
            w_ps = ps.tile([P, 2, P], F32, name="w_ps", tag="a%d" % h)
            words = w[:].bitcast(F32)
            for u in range(2):
                nc.tensor.transpose(w_ps[:, u, :], words[:, u : I // 2 : 2], ident[:])
            if h == 0:
                grouped = reuse.tile([P, P, PACK], BF16, name="w_grouped0", align_bytes=64, offset=16384)
            else:
                grouped = sb.tile([P, P, PACK], BF16, name="w_grouped1", align_bytes=64)
            nc.scalar.copy(out=grouped[:].bitcast(F32), in_=w_ps[:].rearrange("p u q -> p q u"))
            return grouped

        def quantise_weights(h, grouped):
            nc.vector.quantize_mx(
                out=w_codes[:, h * P : (h + 1) * P].bitcast(FP8X4),
                scales=w_scales[:, h * P : (h + 1) * P],
                in_=grouped[:].rearrange("p q t -> p (q t)"),
            )

        wg0 = turn_weights(0)
        wg1 = turn_weights(1)
        t3 = centre_values(3, *g3)
        vg1 = scale_values(1, t1)
        quantise_weights(0, wg0)
        quantise_weights(1, wg1)
        quantise_values(1, vg1)
        vg2 = scale_values(2, t2)
        vg3 = scale_values(3, t3)
        quantise_values(2, vg2)
        quantise_values(3, vg3)

        out_rows = out_0.rearrange("(p j) q -> p j q", j=PACK)

        def product(out, j, cols):
            nc.tensor.matmul_mx(
                out=out,
                lhsT=v_codes[:, j, :].bitcast(FP8X4),
                lhsT_scale=v_scales[:, j, :],
                rhs=w_codes[:, cols].bitcast(FP8X4),
                rhs_scale=w_scales[:, cols],
                start=True,
                stop=True,
            )

        halves = [slice(h * P, (h + 1) * P) for h in range(QT)]
        y_ps = [ps.tile([P, PACK, P], F32, name="y_ps%d" % h, tag="b%d" % h) for h in range(QT)]
        y_pair = [sb.tile([P, 2, Q], F32, name="y_pair%d" % n, align_bytes=64) for n in range(2)]
        for h in range(QT):
            for j in range(2):
                product(y_ps[h][:, j, :], j, halves[h])
            nc.scalar.copy(out=y_pair[0][:, :, halves[h]], in_=y_ps[h][:, 0:2, :])
        nc.sync.dma_start(out=out_rows[:, 0:2, :], in_=y_pair[0][:])
        for j in range(2, PACK):
            for h in range(QT):
                product(y_ps[h][:, j, :], j, halves[h])

        y_grouped = [sb.tile([P, P, PACK], BF16, name="y_grouped%d" % h, align_bytes=64) for h in range(QT)]
        nc.vector.tensor_copy(out=y_grouped[0][:], in_=y_ps[0][:].rearrange("p j q -> p q j"))
        nc.scalar.copy(out=y_grouped[1][:], in_=y_ps[1][:].rearrange("p j q -> p q j"))
        for h in range(QT):
            nc.scalar.copy(out=y_pair[1][:, :, halves[h]], in_=y_ps[h][:, 2:PACK, :])
        nc.scalar.dma_start(out=out_rows[:, 2:PACK, :], in_=y_pair[1][:])
        y_codes = sb.tile([P, Q], U32, name="y_codes", align_bytes=64)
        y_scales = sb.tile([P, Q], U8, name="y_scales", align_bytes=64)
        for h in range(QT):
            nc.vector.quantize_mx(
                out=y_codes[:, halves[h]].bitcast(FP8X4),
                scales=y_scales[:, halves[h]],
                in_=y_grouped[h][:].rearrange("p q j -> p (q j)"),
            )
        nc.sync.dma_start(
            out=out_1[0].rearrange("p q r -> p (q r)").bitcast(I32), in_=y_codes[:].bitcast(I32)
        )
        for quad in range(4):
            queue = nc.scalar if quad % 2 == 0 else nc.sync
            queue.dma_start(
                out=out_2[0, 4 * quad : 4 * quad + 4, :].bitcast(I32),
                in_=y_scales[32 * quad : 32 * quad + 4, :].bitcast(I32),
            )
